import numpy as np
import ml_dtypes


def mxq(x, axis, fmt="e4m3"):
    dtype, down = {"e4m3": (ml_dtypes.float8_e4m3fn, 7), "e5m2": (ml_dtypes.float8_e5m2, 14)}[fmt]
    v = np.moveaxis(np.asarray(x, np.float32).astype(ml_dtypes.bfloat16).astype(np.float64), axis, -1)
    blocks = v.reshape(v.shape[:-1] + (-1, 32))
    amax = np.abs(blocks).max(-1, keepdims=True)
    byte = np.maximum(np.where(amax > 0, np.frexp(amax)[1] - 1 + 127, 0) - down, 1)
    scale = np.exp2(byte - 127.0)
    codes = (blocks / scale).astype(np.float32).astype(dtype).astype(np.float64)
    return np.moveaxis((codes * scale).reshape(v.shape), -1, axis)


WIDE = False


def mx_kscale(k):
    if not WIDE:
        return np.ones(k)
    levels = np.array([10, -10, 5, -5, 0])
    if k % 512:
        return np.exp2(np.random.permutation(np.resize(levels, k // 32))).repeat(32)
    a = np.empty((k // 512, 16))
    for p in range(k // 512):
        a[p, :8] = np.random.permutation(np.resize(levels, 8))
        for g in range(8):
            far = levels[np.abs(levels - a[p, g]) >= 10]
            a[p, g + 8] = far[np.random.randint(len(far))]
    return np.exp2(a.ravel()).repeat(32)


def f64(x):
    return np.asarray(x).astype(np.float64)


def striped(idx):
    return np.tile(idx.reshape(-1, 16).T, (8, 1)).astype(np.uint16)


def unstriped(offs):
    return offs[:16].T.reshape(-1).astype(np.int64)


E2M1 = np.array([0.0, 0.5, 1.0, 1.5, 2.0, 3.0, 4.0, 6.0, -0.0, -0.5, -1.0, -1.5, -2.0, -3.0, -4.0, -6.0])


def pack_weight(w, fmt):
    k, n = w.shape
    w = f64(np.asarray(w, np.float32).astype(ml_dtypes.bfloat16)).reshape(k // 32, 32, n)
    amax = np.abs(w).max(1)
    if fmt == "e4m3":
        byte = np.frexp(amax)[1] - 1 + 127 - 7
    else:
        mant, ex = np.frexp(amax / 6.0)
        byte = np.where(mant > 0.5, ex, ex - 1) + 127
    byte = np.clip(np.where(amax > 0, byte, 1), 1, 254)
    scaled = (w * np.exp2(127.0 - byte)[:, None, :]).reshape(k, n).astype(np.float32)
    by_word = np.ascontiguousarray(scaled.reshape(k // 512, 128, 4, n).transpose(0, 1, 3, 2))
    if fmt == "e4m3":
        words = by_word.astype(ml_dtypes.float8_e4m3fn).view(np.uint8)
    else:
        c = by_word.astype(ml_dtypes.float4_e2m1fn).view(np.uint8) & 0xF
        words = (c[..., 0::2] | (c[..., 1::2] << 4)).reshape(k // 512, 128, 2 * n)
    return np.ascontiguousarray(words), np.ascontiguousarray(byte.astype(np.uint8).reshape(k // 512, 16, n))


def unpack_weight(words, scales, fmt):
    g, _, n = scales.shape
    words = np.ascontiguousarray(words).reshape(g, 128, n, -1)
    if fmt == "e4m3":
        vals = words.view(ml_dtypes.float8_e4m3fn).astype(np.float64)
    else:
        nib = np.empty((g, 128, n, 4), np.uint8)
        nib[..., 0::2] = words & 0xF
        nib[..., 1::2] = words >> 4
        vals = E2M1[nib]
    vals = vals * np.repeat(np.exp2(scales.astype(np.float64) - 127.0), 8, axis=1)[..., None]
    return vals.transpose(0, 1, 3, 2).reshape(g * 512, n)


def gelu(v):
    return 0.5 * v * (1.0 + np.tanh(np.sqrt(2.0 / np.pi) * (v + 0.044715 * v**3)))


def striped8(idx):
    return np.concatenate([v.reshape(-1, 16).T for v in idx]).astype(np.uint16)


def unstriped8(offs):
    return np.stack([offs[16 * g:16 * g + 16].T.reshape(-1) for g in range(8)]).astype(np.int64)


def heads(h, wgt, idx8):
    r = np.arange(h.shape[0])
    return wgt[r // 4 % 128] * h[r[:, None], idx8[r % 512 // 64]]


def put_heads(h, wgs, idx8, t2):
    r = np.arange(h.shape[0])
    page = np.zeros((h.shape[0], t2))
    page[r[:, None], idx8[r % 512 // 64]] = wgs[r // 4 % 128] * h
    return page


K, T, S, H, P, N, T2 = 1536, 4096, 1024, 512, 512, 1024, 1024

def setup_inputs():
    n = np.random.standard_normal
    s = mx_kscale(K)[:, None]
    u = mx_kscale(H)[:, None]
    d = {}
    d["tab_words"], d["tab_scales"] = pack_weight(n((K, T)) * s, "e4m3")
    d["offs"] = striped(np.random.permutation(T)[:S])
    d["w1"] = (n((K, H)) / s * u.T / K**0.5).astype(np.float32)
    d["w2_words"], d["w2_scales"] = pack_weight(n((K, H)) / s / K**0.5, "e2m1")
    d["offs2"] = striped8(np.stack([np.random.permutation(S)[:P] for _ in range(8)]))
    d["wgt"] = np.repeat(np.random.uniform(0.5, 2.0, (8, P)), 16, axis=0).astype(np.float32)
    d["shift"] = (0.7 * n(H) * u[:, 0]).astype(np.float32)
    d["w3"] = (n((H, N)) / u / H**0.5).astype(np.float32)
    d["client"] = (n((K, P)) * s).astype(np.float32)
    d["w4_words"], d["w4_scales"] = pack_weight(n((K, N)) / s / K**0.5, "e2m1")
    d["offs3"] = striped8(np.stack([np.random.permutation(T2)[:P] for _ in range(8)]))
    d["wgo"] = np.repeat(np.random.uniform(0.5, 2.0, (8, P)), 16, axis=0).astype(np.float32)
    return d

def reference(tab_words, tab_scales, offs, w1, w2_words, w2_scales, offs2, wgt, shift, w3, client, w4_words, w4_scales, offs3, wgo):
    v = unpack_weight(tab_words, tab_scales, "e4m3")[:, unstriped(offs)]
    w2 = unpack_weight(w2_words, w2_scales, "e2m1")
    w4 = unpack_weight(w4_words, w4_scales, "e2m1")
    a = mxq(f64(w1), 0, "e4m3").T @ v
    b = w2.T @ v
    h = a * np.exp(-np.square(b))
    x = heads(h, f64(wgt), unstriped8(offs2)) + f64(shift)[:, None]
    filed = mxq(f64(w3), 0, "e4m3").T @ mxq(x, 0, "e4m3")
    own = w4.T @ mxq(f64(client), 0, "e4m3")
    y = np.maximum(filed, own)
    return put_heads(y, f64(wgo), unstriped8(offs3), T2)

@@ -1,0 +1,332 @@
+from contextlib import ExitStack
+
+import concourse.mybir as mybir
+
+K, T, S, H, M, N, T2 = 1536, 4096, 1024, 512, 512, 1024, 1024
+FLOPS = 2 * (2 * K * H * S + H * N * M + K * N * M)
+
+F32 = mybir.dt.float32
+BF16 = mybir.dt.bfloat16
+I32 = mybir.dt.int32
+U32 = mybir.dt.uint32
+U16 = mybir.dt.uint16
+U8 = mybir.dt.uint8
+FP8X4 = mybir.dt.float8_e4m3fn_x4
+FP4X4 = mybir.dt.float4_e2m1fn_x4
+ACT = mybir.ActivationFunctionType
+ALU = mybir.AluOpType
+
+P = 128
+PACK = 4
+KP = P * PACK
+PASSES = K // KP
+BANK = 512
+HALF = M // 2
+QUADS = 4
+LIVE = 100
+KIB = 1024
+
+
+def tile_list_logo_watch_docket_kernel(
+    tc, tab_words, tab_scales, offs, w1, w2_words, w2_scales, offs2, wgt, shift, w3, client,
+    w4_words, w4_scales, offs3, wgo, out,
+):
+    nc = tc.nc
+    with ExitStack() as ctx:
+        keep = ctx.enter_context(tc.tile_pool(name="keep", bufs=1))
+        early = ctx.enter_context(tc.tile_pool(name="early", bufs=1))
+        psum = ctx.enter_context(tc.psum_pool(name="psum", bufs=1))
+
+        def held(shape, dtype, name, bufs=1, tag=None):
+            return keep.tile(shape, dtype, name=name, tag=tag or name, bufs=bufs, align_bytes=64)
+
+        def bank(n, width):
+            return psum.tile([P, width], F32, name=f"bank{n}", tag=f"bank{n}")
+
+        def unpack_planes(queue, engine, packed, first_row, passes, name):
+            planes = {}
+            for a in passes:
+                planes[a] = held(list(packed.shape), U8, f"{name}{a}")
+                engine.memset(planes[a][96:P, :].bitcast(I32), 0)
+                first = first_row + 4 * a
+                queue.dma_start(
+                    out=planes[a][0:LIVE, :].bitcast(I32), in_=packed[first : first + LIVE, :].bitcast(I32)
+                )
+            return planes
+
+        def deal(copy, dst, src, run):
+            copy(
+                out=dst.rearrange("p (t c k) -> p c t k", t=PACK, k=run),
+                in_=src.rearrange("p (c k t) -> p c t k", t=PACK, k=run),
+            )
+
+        def round_dealt(copy, dst, raw):
+            copy(
+                out=dst[:].rearrange("p (t m j) -> p m t j", t=PACK, j=PACK),
+                in_=raw[:].rearrange("p j (m t) -> p m t j", t=PACK),
+            )
+
+        def weave(copy, dst, planes):
+            copy(
+                out=dst.rearrange("p (c k j) -> p c j k", k=4, j=PACK),
+                in_=planes.rearrange("p j (c k) -> p c j k", k=4),
+            )
+
+        def quantise(codes, scales, values):
+            nc.vector.quantize_mx(out=codes.bitcast(FP8X4), scales=scales, in_=values)
+
+        def placed(shape, dtype, name, kib):
+            return early.tile(shape, dtype, name=name, offset=int(kib * KIB), align_bytes=64)
+
+        def load_table(a):
+            words = placed([P, T], U32, f"tab_w{a}", 16 * a)
+            nc.sync.dma_start(
+                out=words[:].bitcast(I32), in_=tab_words[a].rearrange("p t i -> p (t i)").bitcast(I32)
+            )
+            return words
+
+        idx = keep.tile([P, S // 16], U16, name="idx")
+        nc.sync.dma_start(idx[:], offs)
+        idx2 = keep.tile([P, M // 16], U16, name="idx2")
+        nc.sync.dma_start(idx2[:], offs2)
+        tab_w = [load_table(0)]
+        idx3 = keep.tile([P, M // 16], U16, name="idx3")
+        nc.sync.dma_start(idx3[:], offs3)
+        w2_raw = placed([P, PASSES, 2 * H], U8, "w2_raw", 32)
+        nc.sync.dma_start(out=w2_raw[:].bitcast(I32), in_=w2_words.rearrange("a p c -> p a c").bitcast(I32))
+        tab_w.append(load_table(1))
+        tab_s = placed([P, T], U8, "tab_s", 51.5)
+        nc.vector.memset(tab_s[:].bitcast(I32), 0)
+        for q in range(QUADS):
+            nc.scalar.dma_start(
+                out=tab_s[32 * q : 32 * q + 4 * PASSES, :].bitcast(I32),
+                in_=tab_scales[:, 4 * q : 4 * q + 4, :].bitcast(I32),
+            )
+
+        w2_s_raw = held([P, PASSES, H], U8, "w2_s_raw")
+        nc.gpsimd.memset(w2_s_raw[:].bitcast(I32), 0)
+        for q in range(QUADS):
+            nc.gpsimd.dma_start(
+                out=w2_s_raw[32 * q : 32 * q + 4, :, :].bitcast(I32),
+                in_=w2_scales[:, 4 * q : 4 * q + 4, :].rearrange("a r n -> r a n").bitcast(I32),
+            )
+        w4_s_raw = held([P, N], U8, "w4_s_raw")
+        nc.gpsimd.memset(w4_s_raw[:].bitcast(I32), 0)
+        for q in range(QUADS):
+            nc.gpsimd.dma_start(
+                out=w4_s_raw[32 * q : 32 * q + 4 * PASSES, :].bitcast(I32),
+                in_=w4_scales[:, 4 * q : 4 * q + 4, :].bitcast(I32),
+            )
+
+        v_s_packed = held([P, S], U8, "v_s_packed")
+        nc.vector.tensor_copy(v_s_packed[:], tab_s[:].indirect(idx[:]))
+        v_s = unpack_planes(nc.gpsimd, nc.vector, v_s_packed, 0, range(1, PASSES), "v_s")
+        v_s[0] = v_s_packed
+        w2_w = held([P, PASSES, 2 * H], U8, "w2_w")
+        w2_s = placed([P, PASSES, H], U8, "w2_s", 52)
+        w4_s0 = placed([P, N], U8, "w4_s0", 53.5)
+        for a in range(PASSES):
+            deal(nc.scalar.copy, w2_w[:, a, :].bitcast(U16), w2_raw[:, a, :].bitcast(U16), 8)
+        tab_w.append(load_table(2))
+        v_w = [placed([P, S], U32, f"v_w{a}", (48, 54.5, 58.5)[a]) for a in range(PASSES)]
+
+        def gather_words(a):
+            for c in range(2):
+                nc.vector.tensor_copy(
+                    v_w[a][:, c * BANK : (c + 1) * BANK],
+                    tab_w[a][:].indirect(idx[:, c * BANK // 16 : (c + 1) * BANK // 16]),
+                )
+
+        gather_words(0)
+        for a in range(PASSES):
+            deal(nc.vector.tensor_copy, w2_s[:, a, :], w2_s_raw[:, a, :], 16)
+        gather_words(1)
+        gather_words(2)
+        for b in range(2):
+            deal(nc.vector.tensor_copy, w4_s0[:, b * KP : (b + 1) * KP], w4_s_raw[:, b * KP : (b + 1) * KP], 16)
+        w4_s = unpack_planes(nc.gpsimd, nc.vector, w4_s0, 0, range(1, PASSES), "w4_s")
+        w4_s[0] = w4_s0
+        pages = {}
+        for i in range(PACK):
+            pages[0, i] = held([P, T2], F32, f"page0{i}")
+            nc.vector.memset(pages[0, i][:], 0.0)
+
+        w1_raw = []
+        for a in range(PASSES):
+            raw = early.tile([P, PACK, H], F32, name=f"w1_raw{a}", offset=8 * KIB * a)
+            nc.sync.dma_start(out=raw[:], in_=w1[a * KP : (a + 1) * KP, :].rearrange("(p j) c -> p j c", j=PACK))
+            w1_raw.append(raw)
+        wgt_sb = early.tile([P, M], F32, name="wgt_sb", offset=24 * KIB)
+        nc.sync.dma_start(out=wgt_sb[:], in_=wgt)
+        shift_sb = placed([P, PACK], F32, "shift_sb", 29)
+        nc.sync.dma_start(out=shift_sb[:], in_=shift.rearrange("(p i) -> p i", i=PACK))
+
+        slots = [(i, c) for i in range(PACK) for c in range(2)]
+        acc = {(i, c): bank(2 * i + c, BANK) for i, c in slots}
+        for a in range(PASSES):
+            for c in range(2):
+                for i in range(PACK):
+                    nc.tensor.matmul_mx(
+                        out=acc[i, c][:],
+                        lhsT=w2_w[:, a, 2 * P * i : 2 * P * (i + 1)].bitcast(FP4X4),
+                        lhsT_scale=w2_s[:, a, P * i : P * (i + 1)],
+                        rhs=v_w[a][:, c * BANK : (c + 1) * BANK].bitcast(FP8X4),
+                        rhs_scale=v_s[a][:, c * BANK : (c + 1) * BANK],
+                        start=(a == 0), stop=(a == PASSES - 1),
+                    )
+        h = []
+        for i in range(PACK):
+            square = held([P, S], F32, "square", bufs=2)
+            for c in range(2):
+                nc.scalar.activation(out=square[:, c * BANK : (c + 1) * BANK], in_=acc[i, c][:], func=ACT.Square)
+            rows = held([P, S], F32, f"h{i}")
+            nc.scalar.activation(out=rows[:], in_=square[:], func=ACT.Exp, scale=-1.0)
+            h.append(rows)
+
+        w1_w = held([P, PASSES, H], U32, "w1_w")
+        w1_s = held([P, PASSES, H], U8, "w1_s")
+        acc = {(i, c): bank(2 * i + c, BANK) for i, c in slots}
+        for a in range(PASSES):
+            rounded = held([P, PACK * H], BF16, "w1_bf", bufs=2)
+            round_dealt(nc.vector.tensor_copy, rounded, w1_raw[a])
+            for i in range(PACK):
+                cols = slice(P * i, P * (i + 1))
+                quantise(w1_w[:, a, cols], w1_s[:, a, cols], rounded[:, KP * i : KP * (i + 1)])
+            for i, c in slots:
+                cols = slice(P * i, P * (i + 1))
+                nc.tensor.matmul_mx(
+                    out=acc[i, c][:],
+                    lhsT=w1_w[:, a, cols].bitcast(FP8X4),
+                    lhsT_scale=w1_s[:, a, cols],
+                    rhs=v_w[a][:, c * BANK : (c + 1) * BANK].bitcast(FP8X4),
+                    rhs_scale=v_s[a][:, c * BANK : (c + 1) * BANK],
+                    start=(a == 0), stop=(a == PASSES - 1),
+                )
+
+        w4_raw, w3_raw, client_raw = {}, {}, {}
+
+        def load_w4(b):
+            w4_raw[b] = early.tile([P, PASSES, 2 * KP], U8, name=f"w4_raw{b}", offset=KIB * (26, 40)[b])
+            nc.sync.dma_start(
+                out=w4_raw[b][:].bitcast(I32),
+                in_=w4_words.rearrange("a p c -> p a c")[:, :, 2 * KP * b : 2 * KP * (b + 1)].bitcast(I32),
+            )
+
+        def load_client(s):
+            for a in range(PASSES):
+                client_raw[a, s] = early.tile(
+                    [P, PACK, HALF], F32, name=f"client_raw{a}{s}", offset=KIB * ((32, 8)[s] + 4 * a)
+                )
+                rows_k = client[a * KP : (a + 1) * KP, s * HALF : (s + 1) * HALF]
+                nc.sync.dma_start(out=client_raw[a, s][:], in_=rows_k.rearrange("(p j) m -> p j m", j=PACK))
+
+        def load_w3(b):
+            w3_raw[b] = early.tile([P, PACK, KP], F32, name=f"w3_raw{b}", offset=KIB * (0, 32)[b])
+            nc.sync.dma_start(
+                out=w3_raw[b][:], in_=w3[:, b * KP : (b + 1) * KP].rearrange("(p j) n -> p j n", j=PACK)
+            )
+
+        load_w4(0)
+        load_client(0)
+        load_w3(0)
+        wgo_sb = early.tile([P, M], F32, name="wgo_sb", offset=44 * KIB)
+        nc.sync.dma_start(out=wgo_sb[:], in_=wgo)
+        load_client(1)
+
+        w4_w = held([P, 2, PASSES, 2 * KP], U8, "w4_w")
+        w3_w = held([P, N], U32, "w3_w")
+        w3_s = held([P, N], U8, "w3_s")
+        client_w = held([P, PASSES, M], U32, "client_w")
+        client_s = held([P, PASSES, M], U8, "client_s")
+        x_w = held([P, M], U32, "x_w")
+        x_s = held([P, M], U8, "x_s")
+
+        def prepare_w4(b):
+            for a in range(PASSES):
+                deal(nc.scalar.copy, w4_w[:, b, a, :].bitcast(U16), w4_raw[b][:, a, :].bitcast(U16), 8)
+
+        def prepare_client(s):
+            cols = slice(s * HALF, (s + 1) * HALF)
+            for a in range(PASSES):
+                rounded = held([P, PACK * HALF], BF16, f"client_bf{a}{s}")
+                weave(nc.scalar.copy, rounded[:], client_raw[a, s][:])
+                quantise(client_w[:, a, cols], client_s[:, a, cols], rounded[:])
+
+        def prepare_w3(b, copy):
+            cols = slice(b * KP, (b + 1) * KP)
+            rounded = held([P, PACK * KP], BF16, f"w3_bf{b}")
+            round_dealt(copy, rounded, w3_raw[b])
+            quantise(w3_w[:, cols], w3_s[:, cols], rounded[:])
+
+        x_planes = [held([P, PACK, HALF], BF16, f"x_planes{s}") for s in range(2)]
+        for i in range(PACK):
+            for c in range(2):
+                cols = slice(c * BANK, (c + 1) * BANK)
+                nc.vector.tensor_tensor(out=h[i][:, cols], in0=acc[i, c][:], in1=h[i][:, cols], op=ALU.mult)
+            for s in range(2):
+                picked = held([P, HALF], F32, f"picked{i}{s}")
+                nc.vector.tensor_tensor(
+                    picked[:],
+                    h[i][:].indirect(idx2[:, s * HALF // 16 : (s + 1) * HALF // 16]),
+                    wgt_sb[:, s * HALF : (s + 1) * HALF],
+                    ALU.mult,
+                )
+                nc.scalar.activation(
+                    out=x_planes[s][:, i, :], in_=picked[:], func=ACT.Identity, bias=shift_sb[:, i : i + 1]
+                )
+        prepare_w4(0)
+        prepare_client(0)
+        load_w3(1)
+        load_w4(1)
+        prepare_w3(0, nc.vector.tensor_copy)
+        for s in range(2):
+            cols = slice(s * HALF, (s + 1) * HALF)
+            x_bf = held([P, PACK * HALF], BF16, f"x_bf{s}")
+            weave(nc.vector.tensor_copy, x_bf[:], x_planes[s][:])
+            quantise(x_w[:, cols], x_s[:, cols], x_bf[:])
+
+        out_rows = out.rearrange("(b p i) c -> b i p c", b=2, i=PACK)
+
+        def enter(b, i, m0, width, own_sb):
+            cols = slice(m0, m0 + width)
+            n_cols = slice(b * KP + P * i, b * KP + P * (i + 1))
+            own = bank(i, width)
+            for a in range(PASSES):
+                nc.tensor.matmul_mx(
+                    out=own[:],
+                    lhsT=w4_w[:, b, a, 2 * P * i : 2 * P * (i + 1)].bitcast(FP4X4),
+                    lhsT_scale=w4_s[a][:, n_cols],
+                    rhs=client_w[:, a, cols].bitcast(FP8X4),
+                    rhs_scale=client_s[:, a, cols],
+                    start=(a == 0), stop=(a == PASSES - 1),
+                )
+            nc.scalar.copy(out=own_sb[:], in_=own[:])
+            filed = bank(PACK + i, width)
+            nc.tensor.matmul_mx(
+                out=filed[:],
+                lhsT=w3_w[:, n_cols].bitcast(FP8X4), lhsT_scale=w3_s[:, n_cols],
+                rhs=x_w[:, cols].bitcast(FP8X4), rhs_scale=x_s[:, cols],
+                start=True, stop=True,
+            )
+            y = held([P, width], F32, "y", bufs=3)
+            nc.vector.tensor_tensor(out=y[:], in0=filed[:], in1=own_sb[:], op=ALU.max)
+            nc.vector.tensor_tensor(
+                pages[b, i][:].indirect(idx3[:, m0 // 16 : (m0 + width) // 16]), y[:], wgo_sb[:, cols], ALU.mult
+            )
+
+        for s in range(2):
+            if s == 1:
+                prepare_client(1)
+            for i in range(PACK):
+                own_sb = held([P, HALF], F32, f"own0{i}{s}")
+                enter(0, i, s * HALF, HALF, own_sb)
+                if s == 1:
+                    nc.sync.dma_start(out=out_rows[0, i], in_=pages[0, i][:])
+        prepare_w4(1)
+        prepare_w3(1, nc.scalar.copy)
+        for i in range(PACK):
+            pages[1, i] = early.tile([P, T2], F32, name=f"page1{i}", offset=KIB * (8 + 4 * i if i < 3 else 32))
+            nc.gpsimd.memset(pages[1, i][:], 0.0)
+            own_sb = early.tile([P, M], F32, name=f"own1{i}", offset=2 * KIB * i)
+            enter(1, i, 0, M, own_sb)
+            nc.sync.dma_start(out=out_rows[1, i], in_=pages[1, i][:])

@@ -68,8 +68,8 @@ def tile_list_logo_watch_docket_kernel(
 
         def weave(copy, dst, planes):
             copy(
-                out=dst.rearrange("p (c k j) -> p c j k", k=4, j=PACK),
-                in_=planes.rearrange("p j (c k) -> p c j k", k=4),
+                out=dst.rearrange("p (m j) -> p m j", j=PACK),
+                in_=planes.rearrange("p j m -> p m j"),
             )
 
         def quantise(codes, scales, values):
@@ -89,13 +89,20 @@ def tile_list_logo_watch_docket_kernel(
         nc.sync.dma_start(idx[:], offs)
         idx2 = keep.tile([P, M // 16], U16, name="idx2")
         nc.sync.dma_start(idx2[:], offs2)
-        tab_w = [load_table(0)]
         idx3 = keep.tile([P, M // 16], U16, name="idx3")
         nc.sync.dma_start(idx3[:], offs3)
-        w2_raw = placed([P, PASSES, 2 * H], U8, "w2_raw", 32)
+        tab_w = [load_table(0)]
+        w2_raw = held([P, PASSES, 2 * H], U8, "w2_raw")
         nc.sync.dma_start(out=w2_raw[:].bitcast(I32), in_=w2_words.rearrange("a p c -> p a c").bitcast(I32))
         tab_w.append(load_table(1))
-        tab_s = placed([P, T], U8, "tab_s", 51.5)
+
+        def load_w1(a):
+            raw = placed([P, PACK, H], F32, f"w1_raw{a}", (62.5, 0, 8)[a])
+            nc.sync.dma_start(out=raw[:], in_=w1[a * KP : (a + 1) * KP, :].rearrange("(p j) c -> p j c", j=PACK))
+            return raw
+
+        w1_raw = [load_w1(0)]
+        tab_s = placed([P, T], U8, "tab_s", 47.5)
         nc.vector.memset(tab_s[:].bitcast(I32), 0)
         for q in range(QUADS):
             nc.scalar.dma_start(
@@ -103,7 +110,7 @@ def tile_list_logo_watch_docket_kernel(
                 in_=tab_scales[:, 4 * q : 4 * q + 4, :].bitcast(I32),
             )
 
-        w2_s_raw = held([P, PASSES, H], U8, "w2_s_raw")
+        w2_s_raw = placed([P, PASSES, H], U8, "w2_s_raw", 56)
         nc.gpsimd.memset(w2_s_raw[:].bitcast(I32), 0)
         for q in range(QUADS):
             nc.gpsimd.dma_start(
@@ -120,15 +127,15 @@ def tile_list_logo_watch_docket_kernel(
 
         v_s_packed = held([P, S], U8, "v_s_packed")
         nc.vector.tensor_copy(v_s_packed[:], tab_s[:].indirect(idx[:]))
-        v_s = unpack_planes(nc.gpsimd, nc.vector, v_s_packed, 0, range(1, PASSES), "v_s")
+        v_s = unpack_planes(nc.sync, nc.vector, v_s_packed, 0, range(1, PASSES), "v_s")
         v_s[0] = v_s_packed
         w2_w = held([P, PASSES, 2 * H], U8, "w2_w")
-        w2_s = placed([P, PASSES, H], U8, "w2_s", 52)
-        w4_s0 = placed([P, N], U8, "w4_s0", 53.5)
+        w2_s = placed([P, PASSES, H], U8, "w2_s", 48)
+        w4_s0 = placed([P, N], U8, "w4_s0", 49.5)
         for a in range(PASSES):
             deal(nc.scalar.copy, w2_w[:, a, :].bitcast(U16), w2_raw[:, a, :].bitcast(U16), 8)
         tab_w.append(load_table(2))
-        v_w = [placed([P, S], U32, f"v_w{a}", (48, 54.5, 58.5)[a]) for a in range(PASSES)]
+        v_w = [placed([P, S], U32, f"v_w{a}", 50.5 + 4 * a) for a in range(PASSES)]
 
         def gather_words(a):
             for c in range(2):
@@ -149,14 +156,13 @@ def tile_list_logo_watch_docket_kernel(
         pages = {}
         for i in range(PACK):
             pages[0, i] = held([P, T2], F32, f"page0{i}")
-            nc.vector.memset(pages[0, i][:], 0.0)
+            nc.vector.memset(pages[0, i][:, 0 : T2 - 1], 0.0)
+            nc.vector.memset(pages[0, i][:, T2 - 1 : T2], 0.0)
+            pages[1, i] = held([P, T2], F32, f"page1{i}")
+            nc.gpsimd.memset(pages[1, i][:], 0.0)
 
-        w1_raw = []
-        for a in range(PASSES):
-            raw = early.tile([P, PACK, H], F32, name=f"w1_raw{a}", offset=8 * KIB * a)
-            nc.sync.dma_start(out=raw[:], in_=w1[a * KP : (a + 1) * KP, :].rearrange("(p j) c -> p j c", j=PACK))
-            w1_raw.append(raw)
-        wgt_sb = early.tile([P, M], F32, name="wgt_sb", offset=24 * KIB)
+        w1_raw.extend(load_w1(a) for a in range(1, PASSES))
+        wgt_sb = early.tile([P, M], F32, name="wgt_sb", offset=16 * KIB)
         nc.sync.dma_start(out=wgt_sb[:], in_=wgt)
         shift_sb = placed([P, PACK], F32, "shift_sb", 29)
         nc.sync.dma_start(out=shift_sb[:], in_=shift.rearrange("(p i) -> p i", i=PACK))
@@ -206,7 +212,7 @@ def tile_list_logo_watch_docket_kernel(
         w4_raw, w3_raw, client_raw = {}, {}, {}
 
         def load_w4(b):
-            w4_raw[b] = early.tile([P, PASSES, 2 * KP], U8, name=f"w4_raw{b}", offset=KIB * (26, 40)[b])
+            w4_raw[b] = early.tile([P, PASSES, 2 * KP], U8, name=f"w4_raw{b}", offset=KIB * (18, 32)[b])
             nc.sync.dma_start(
                 out=w4_raw[b][:].bitcast(I32),
                 in_=w4_words.rearrange("a p c -> p a c")[:, :, 2 * KP * b : 2 * KP * (b + 1)].bitcast(I32),
@@ -215,13 +221,13 @@ def tile_list_logo_watch_docket_kernel(
         def load_client(s):
             for a in range(PASSES):
                 client_raw[a, s] = early.tile(
-                    [P, PACK, HALF], F32, name=f"client_raw{a}{s}", offset=KIB * ((32, 8)[s] + 4 * a)
+                    [P, PACK, HALF], F32, name=f"client_raw{a}{s}", offset=KIB * ((21, 25, 32), (0, 4, 8))[s][a]
                 )
                 rows_k = client[a * KP : (a + 1) * KP, s * HALF : (s + 1) * HALF]
                 nc.sync.dma_start(out=client_raw[a, s][:], in_=rows_k.rearrange("(p j) m -> p j m", j=PACK))
 
         def load_w3(b):
-            w3_raw[b] = early.tile([P, PACK, KP], F32, name=f"w3_raw{b}", offset=KIB * (0, 32)[b])
+            w3_raw[b] = early.tile([P, PACK, KP], F32, name=f"w3_raw{b}", offset=KIB * (36, 21)[b])
             nc.sync.dma_start(
                 out=w3_raw[b][:], in_=w3[:, b * KP : (b + 1) * KP].rearrange("(p j) n -> p j n", j=PACK)
             )
@@ -325,8 +331,6 @@ def tile_list_logo_watch_docket_kernel(
         prepare_w4(1)
         prepare_w3(1, nc.scalar.copy)
         for i in range(PACK):
-            pages[1, i] = early.tile([P, T2], F32, name=f"page1{i}", offset=KIB * (8 + 4 * i if i < 3 else 32))
-            nc.gpsimd.memset(pages[1, i][:], 0.0)
-            own_sb = early.tile([P, M], F32, name=f"own1{i}", offset=2 * KIB * i)
+            own_sb = early.tile([P, M], F32, name=f"own1{i}", offset=KIB * (36 + 2 * i))
             enter(1, i, 0, M, own_sb)
             nc.sync.dma_start(out=out_rows[1, i], in_=pages[1, i][:])

@@ -43,16 +43,11 @@ def tile_list_logo_watch_docket_kernel(
         def bank(n, width):
             return psum.tile([P, width], F32, name=f"bank{n}", tag=f"bank{n}")
 
-        def unpack_planes(queue, engine, packed, first_row, passes, name):
-            planes = {}
-            for a in passes:
-                planes[a] = held(list(packed.shape), U8, f"{name}{a}")
-                engine.memset(planes[a][96:P, :].bitcast(I32), 0)
-                first = first_row + 4 * a
-                queue.dma_start(
-                    out=planes[a][0:LIVE, :].bitcast(I32), in_=packed[first : first + LIVE, :].bitcast(I32)
-                )
-            return planes
+        def lift_plane(queue, packed, a, name):
+            plane = held(list(packed.shape), U8, f"{name}{a}")
+            nc.vector.memset(plane[96:P, :].bitcast(I32), 0)
+            queue.dma_start(out=plane[0:LIVE, :].bitcast(I32), in_=packed[4 * a : 4 * a + LIVE, :].bitcast(I32))
+            return plane
 
         def deal(copy, dst, src, run):
             copy(
@@ -92,25 +87,20 @@ def tile_list_logo_watch_docket_kernel(
         idx3 = keep.tile([P, M // 16], U16, name="idx3")
         nc.sync.dma_start(idx3[:], offs3)
         tab_w = [load_table(0)]
+        shift_sb = held([P, PACK], F32, "shift_sb")
+        nc.sync.dma_start(out=shift_sb[:], in_=shift.rearrange("(p i) -> p i", i=PACK))
         w2_raw = held([P, PASSES, 2 * H], U8, "w2_raw")
         nc.sync.dma_start(out=w2_raw[:].bitcast(I32), in_=w2_words.rearrange("a p c -> p a c").bitcast(I32))
-        tab_w.append(load_table(1))
-
-        def load_w1(a):
-            raw = placed([P, PACK, H], F32, f"w1_raw{a}", (62.5, 0, 8)[a])
-            nc.sync.dma_start(out=raw[:], in_=w1[a * KP : (a + 1) * KP, :].rearrange("(p j) c -> p j c", j=PACK))
-            return raw
-
-        w1_raw = [load_w1(0)]
         tab_s = placed([P, T], U8, "tab_s", 47.5)
         nc.vector.memset(tab_s[:].bitcast(I32), 0)
         for q in range(QUADS):
-            nc.scalar.dma_start(
+            nc.sync.dma_start(
                 out=tab_s[32 * q : 32 * q + 4 * PASSES, :].bitcast(I32),
                 in_=tab_scales[:, 4 * q : 4 * q + 4, :].bitcast(I32),
             )
+        tab_w.append(load_table(1))
 
-        w2_s_raw = placed([P, PASSES, H], U8, "w2_s_raw", 56)
+        w2_s_raw = held([P, PASSES, H], U8, "w2_s_raw")
         nc.gpsimd.memset(w2_s_raw[:].bitcast(I32), 0)
         for q in range(QUADS):
             nc.gpsimd.dma_start(
@@ -127,14 +117,12 @@ def tile_list_logo_watch_docket_kernel(
 
         v_s_packed = held([P, S], U8, "v_s_packed")
         nc.vector.tensor_copy(v_s_packed[:], tab_s[:].indirect(idx[:]))
-        v_s = unpack_planes(nc.sync, nc.vector, v_s_packed, 0, range(1, PASSES), "v_s")
-        v_s[0] = v_s_packed
         w2_w = held([P, PASSES, 2 * H], U8, "w2_w")
         w2_s = placed([P, PASSES, H], U8, "w2_s", 48)
-        w4_s0 = placed([P, N], U8, "w4_s0", 49.5)
         for a in range(PASSES):
             deal(nc.scalar.copy, w2_w[:, a, :].bitcast(U16), w2_raw[:, a, :].bitcast(U16), 8)
         tab_w.append(load_table(2))
+        v_s = [v_s_packed] + [lift_plane(nc.sync, v_s_packed, a, "v_s") for a in range(1, PASSES)]
         v_w = [placed([P, S], U32, f"v_w{a}", 50.5 + 4 * a) for a in range(PASSES)]
 
         def gather_words(a):
@@ -149,10 +137,10 @@ def tile_list_logo_watch_docket_kernel(
             deal(nc.vector.tensor_copy, w2_s[:, a, :], w2_s_raw[:, a, :], 16)
         gather_words(1)
         gather_words(2)
+        w4_s0 = placed([P, N], U8, "w4_s0", 46)
         for b in range(2):
             deal(nc.vector.tensor_copy, w4_s0[:, b * KP : (b + 1) * KP], w4_s_raw[:, b * KP : (b + 1) * KP], 16)
-        w4_s = unpack_planes(nc.gpsimd, nc.vector, w4_s0, 0, range(1, PASSES), "w4_s")
-        w4_s[0] = w4_s0
+        w4_s = [w4_s0] + [lift_plane(nc.gpsimd, w4_s0, a, "w4_s") for a in range(1, PASSES)]
         pages = {}
         for i in range(PACK):
             pages[0, i] = held([P, T2], F32, f"page0{i}")
@@ -161,25 +149,26 @@ def tile_list_logo_watch_docket_kernel(
             pages[1, i] = held([P, T2], F32, f"page1{i}")
             nc.gpsimd.memset(pages[1, i][:], 0.0)
 
-        w1_raw.extend(load_w1(a) for a in range(1, PASSES))
-        wgt_sb = early.tile([P, M], F32, name="wgt_sb", offset=16 * KIB)
+        w1_raw = []
+        for a in range(PASSES):
+            raw = early.tile([P, PACK, H], F32, name=f"w1_raw{a}", offset=8 * KIB * a)
+            nc.sync.dma_start(out=raw[:], in_=w1[a * KP : (a + 1) * KP, :].rearrange("(p j) c -> p j c", j=PACK))
+            w1_raw.append(raw)
+        wgt_sb = early.tile([P, M], F32, name="wgt_sb", offset=24 * KIB)
         nc.sync.dma_start(out=wgt_sb[:], in_=wgt)
-        shift_sb = placed([P, PACK], F32, "shift_sb", 29)
-        nc.sync.dma_start(out=shift_sb[:], in_=shift.rearrange("(p i) -> p i", i=PACK))
 
         slots = [(i, c) for i in range(PACK) for c in range(2)]
         acc = {(i, c): bank(2 * i + c, BANK) for i, c in slots}
-        for a in range(PASSES):
-            for c in range(2):
-                for i in range(PACK):
-                    nc.tensor.matmul_mx(
-                        out=acc[i, c][:],
-                        lhsT=w2_w[:, a, 2 * P * i : 2 * P * (i + 1)].bitcast(FP4X4),
-                        lhsT_scale=w2_s[:, a, P * i : P * (i + 1)],
-                        rhs=v_w[a][:, c * BANK : (c + 1) * BANK].bitcast(FP8X4),
-                        rhs_scale=v_s[a][:, c * BANK : (c + 1) * BANK],
-                        start=(a == 0), stop=(a == PASSES - 1),
-                    )
+        for a, c in [(0, c) for c in range(2)] + [(a, c) for c in range(2) for a in range(1, PASSES)]:
+            for i in range(PACK):
+                nc.tensor.matmul_mx(
+                    out=acc[i, c][:],
+                    lhsT=w2_w[:, a, 2 * P * i : 2 * P * (i + 1)].bitcast(FP4X4),
+                    lhsT_scale=w2_s[:, a, P * i : P * (i + 1)],
+                    rhs=v_w[a][:, c * BANK : (c + 1) * BANK].bitcast(FP8X4),
+                    rhs_scale=v_s[a][:, c * BANK : (c + 1) * BANK],
+                    start=(a == 0), stop=(a == PASSES - 1),
+                )
         h = []
         for i in range(PACK):
             square = held([P, S], F32, "square", bufs=2)
@@ -212,7 +201,7 @@ def tile_list_logo_watch_docket_kernel(
         w4_raw, w3_raw, client_raw = {}, {}, {}
 
         def load_w4(b):
-            w4_raw[b] = early.tile([P, PASSES, 2 * KP], U8, name=f"w4_raw{b}", offset=KIB * (18, 32)[b])
+            w4_raw[b] = early.tile([P, PASSES, 2 * KP], U8, name=f"w4_raw{b}", offset=KIB * (26, 40)[b])
             nc.sync.dma_start(
                 out=w4_raw[b][:].bitcast(I32),
                 in_=w4_words.rearrange("a p c -> p a c")[:, :, 2 * KP * b : 2 * KP * (b + 1)].bitcast(I32),
@@ -221,13 +210,13 @@ def tile_list_logo_watch_docket_kernel(
         def load_client(s):
             for a in range(PASSES):
                 client_raw[a, s] = early.tile(
-                    [P, PACK, HALF], F32, name=f"client_raw{a}{s}", offset=KIB * ((21, 25, 32), (0, 4, 8))[s][a]
+                    [P, PACK, HALF], F32, name=f"client_raw{a}{s}", offset=KIB * ((32, 8)[s] + 4 * a)
                 )
                 rows_k = client[a * KP : (a + 1) * KP, s * HALF : (s + 1) * HALF]
                 nc.sync.dma_start(out=client_raw[a, s][:], in_=rows_k.rearrange("(p j) m -> p j m", j=PACK))
 
         def load_w3(b):
-            w3_raw[b] = early.tile([P, PACK, KP], F32, name=f"w3_raw{b}", offset=KIB * (36, 21)[b])
+            w3_raw[b] = early.tile([P, PACK, KP], F32, name=f"w3_raw{b}", offset=KIB * (0, 32)[b])
             nc.sync.dma_start(
                 out=w3_raw[b][:], in_=w3[:, b * KP : (b + 1) * KP].rearrange("(p j) n -> p j n", j=PACK)
             )
@@ -331,6 +320,6 @@ def tile_list_logo_watch_docket_kernel(
         prepare_w4(1)
         prepare_w3(1, nc.scalar.copy)
         for i in range(PACK):
-            own_sb = early.tile([P, M], F32, name=f"own1{i}", offset=KIB * (36 + 2 * i))
+            own_sb = early.tile([P, M], F32, name=f"own1{i}", offset=2 * KIB * i)
             enter(1, i, 0, M, own_sb)
             nc.sync.dma_start(out=out_rows[1, i], in_=pages[1, i][:])

from contextlib import ExitStack

import concourse.mybir as mybir

K, T, S, H, M, N, T2 = 1536, 4096, 1024, 512, 512, 1024, 1024
FLOPS = 2 * (2 * K * H * S + H * N * M + K * N * M)

F32 = mybir.dt.float32
BF16 = mybir.dt.bfloat16
I32 = mybir.dt.int32
U32 = mybir.dt.uint32
U16 = mybir.dt.uint16
U8 = mybir.dt.uint8
FP8X4 = mybir.dt.float8_e4m3fn_x4
FP4X4 = mybir.dt.float4_e2m1fn_x4
ACT = mybir.ActivationFunctionType
ALU = mybir.AluOpType

P = 128
PACK = 4
KP = P * PACK
PASSES = K // KP
BANK = 512
HALF = M // 2
QUADS = 4
LIVE = 100
KIB = 1024


def tile_list_logo_watch_docket_kernel(
    tc, tab_words, tab_scales, offs, w1, w2_words, w2_scales, offs2, wgt, shift, w3, client,
    w4_words, w4_scales, offs3, wgo, out,
):
    nc = tc.nc
    with ExitStack() as ctx:
        keep = ctx.enter_context(tc.tile_pool(name="keep", bufs=1))
        early = ctx.enter_context(tc.tile_pool(name="early", bufs=1))
        psum = ctx.enter_context(tc.psum_pool(name="psum", bufs=1))

        def held(shape, dtype, name, bufs=1, tag=None):
            return keep.tile(shape, dtype, name=name, tag=tag or name, bufs=bufs, align_bytes=64)

        def bank(n, width):
            return psum.tile([P, width], F32, name=f"bank{n}", tag=f"bank{n}")

        def lift_plane(queue, packed, a, name):
            plane = held(list(packed.shape), U8, f"{name}{a}")
            nc.vector.memset(plane[96:P, :].bitcast(I32), 0)
            queue.dma_start(out=plane[0:LIVE, :].bitcast(I32), in_=packed[4 * a : 4 * a + LIVE, :].bitcast(I32))
            return plane

        def deal(copy, dst, src, run):
            copy(
                out=dst.rearrange("p (t c k) -> p c t k", t=PACK, k=run),
                in_=src.rearrange("p (c k t) -> p c t k", t=PACK, k=run),
            )

        def round_dealt(copy, dst, raw):
            copy(
                out=dst[:].rearrange("p (t m j) -> p m t j", t=PACK, j=PACK),
                in_=raw[:].rearrange("p j (m t) -> p m t j", t=PACK),
            )

        def weave(copy, dst, planes):
            copy(
                out=dst.rearrange("p (m j) -> p m j", j=PACK),
                in_=planes.rearrange("p j m -> p m j"),
            )

        def quantise(codes, scales, values):
            nc.vector.quantize_mx(out=codes.bitcast(FP8X4), scales=scales, in_=values)

        def placed(shape, dtype, name, kib):
            return early.tile(shape, dtype, name=name, offset=int(kib * KIB), align_bytes=64)

        def load_table(a):
            words = placed([P, T], U32, f"tab_w{a}", 16 * a)
            nc.sync.dma_start(
                out=words[:].bitcast(I32), in_=tab_words[a].rearrange("p t i -> p (t i)").bitcast(I32)
            )
            return words

        idx = keep.tile([P, S // 16], U16, name="idx")
        nc.sync.dma_start(idx[:], offs)
        idx2 = keep.tile([P, M // 16], U16, name="idx2")
        nc.sync.dma_start(idx2[:], offs2)
        idx3 = keep.tile([P, M // 16], U16, name="idx3")
        nc.sync.dma_start(idx3[:], offs3)
        tab_w = [load_table(0)]
        shift_sb = held([P, PACK], F32, "shift_sb")
        nc.sync.dma_start(out=shift_sb[:], in_=shift.rearrange("(p i) -> p i", i=PACK))
        w2_raw = held([P, PASSES, 2 * H], U8, "w2_raw")
        nc.sync.dma_start(out=w2_raw[:].bitcast(I32), in_=w2_words.rearrange("a p c -> p a c").bitcast(I32))
        tab_s = placed([P, T], U8, "tab_s", 47.5)
        nc.vector.memset(tab_s[:].bitcast(I32), 0)
        for q in range(QUADS):
            nc.sync.dma_start(
                out=tab_s[32 * q : 32 * q + 4 * PASSES, :].bitcast(I32),
                in_=tab_scales[:, 4 * q : 4 * q + 4, :].bitcast(I32),
            )
        tab_w.append(load_table(1))

        w2_s_raw = held([P, PASSES, H], U8, "w2_s_raw")
        nc.gpsimd.memset(w2_s_raw[:].bitcast(I32), 0)
        for q in range(QUADS):
            nc.gpsimd.dma_start(
                out=w2_s_raw[32 * q : 32 * q + 4, :, :].bitcast(I32),
                in_=w2_scales[:, 4 * q : 4 * q + 4, :].rearrange("a r n -> r a n").bitcast(I32),
            )
        w4_s_raw = held([P, N], U8, "w4_s_raw")
        nc.gpsimd.memset(w4_s_raw[:].bitcast(I32), 0)
        for q in range(QUADS):
            nc.gpsimd.dma_start(
                out=w4_s_raw[32 * q : 32 * q + 4 * PASSES, :].bitcast(I32),
                in_=w4_scales[:, 4 * q : 4 * q + 4, :].bitcast(I32),
            )

        v_s_packed = held([P, S], U8, "v_s_packed")
        nc.vector.tensor_copy(v_s_packed[:], tab_s[:].indirect(idx[:]))
        w2_w = held([P, PASSES, 2 * H], U8, "w2_w")
        w2_s = placed([P, PASSES, H], U8, "w2_s", 48)
        for a in range(PASSES):
            deal(nc.scalar.copy, w2_w[:, a, :].bitcast(U16), w2_raw[:, a, :].bitcast(U16), 8)
        tab_w.append(load_table(2))
        v_s = [v_s_packed] + [lift_plane(nc.sync, v_s_packed, a, "v_s") for a in range(1, PASSES)]
        v_w = [placed([P, S], U32, f"v_w{a}", 50.5 + 4 * a) for a in range(PASSES)]

        def gather_words(a):
            for c in range(2):
                nc.vector.tensor_copy(
                    v_w[a][:, c * BANK : (c + 1) * BANK],
                    tab_w[a][:].indirect(idx[:, c * BANK // 16 : (c + 1) * BANK // 16]),
                )

        gather_words(0)
        for a in range(PASSES):
            deal(nc.vector.tensor_copy, w2_s[:, a, :], w2_s_raw[:, a, :], 16)
        gather_words(1)
        gather_words(2)
        w4_s0 = placed([P, N], U8, "w4_s0", 46)
        for b in range(2):
            deal(nc.vector.tensor_copy, w4_s0[:, b * KP : (b + 1) * KP], w4_s_raw[:, b * KP : (b + 1) * KP], 16)
        w4_s = [w4_s0] + [lift_plane(nc.gpsimd, w4_s0, a, "w4_s") for a in range(1, PASSES)]
        pages = {}
        for i in range(PACK):
            pages[0, i] = held([P, T2], F32, f"page0{i}")
            nc.vector.memset(pages[0, i][:, 0 : T2 - 1], 0.0)
            nc.vector.memset(pages[0, i][:, T2 - 1 : T2], 0.0)
            pages[1, i] = held([P, T2], F32, f"page1{i}")
            nc.gpsimd.memset(pages[1, i][:], 0.0)

        w1_raw = []
        for a in range(PASSES):
            raw = early.tile([P, PACK, H], F32, name=f"w1_raw{a}", offset=8 * KIB * a)
            nc.sync.dma_start(out=raw[:], in_=w1[a * KP : (a + 1) * KP, :].rearrange("(p j) c -> p j c", j=PACK))
            w1_raw.append(raw)
        wgt_sb = early.tile([P, M], F32, name="wgt_sb", offset=24 * KIB)
        nc.sync.dma_start(out=wgt_sb[:], in_=wgt)

        slots = [(i, c) for i in range(PACK) for c in range(2)]
        acc = {(i, c): bank(2 * i + c, BANK) for i, c in slots}
        for a, c in [(0, c) for c in range(2)] + [(a, c) for c in range(2) for a in range(1, PASSES)]:
            for i in range(PACK):
                nc.tensor.matmul_mx(
                    out=acc[i, c][:],
                    lhsT=w2_w[:, a, 2 * P * i : 2 * P * (i + 1)].bitcast(FP4X4),
                    lhsT_scale=w2_s[:, a, P * i : P * (i + 1)],
                    rhs=v_w[a][:, c * BANK : (c + 1) * BANK].bitcast(FP8X4),
                    rhs_scale=v_s[a][:, c * BANK : (c + 1) * BANK],
                    start=(a == 0), stop=(a == PASSES - 1),
                )
        h = []
        for i in range(PACK):
            square = held([P, S], F32, "square", bufs=2)
            for c in range(2):
                nc.scalar.activation(out=square[:, c * BANK : (c + 1) * BANK], in_=acc[i, c][:], func=ACT.Square)
            rows = held([P, S], F32, f"h{i}")
            nc.scalar.activation(out=rows[:], in_=square[:], func=ACT.Exp, scale=-1.0)
            h.append(rows)

        w1_w = held([P, PASSES, H], U32, "w1_w")
        w1_s = held([P, PASSES, H], U8, "w1_s")
        acc = {(i, c): bank(2 * i + c, BANK) for i, c in slots}
        for a in range(PASSES):
            rounded = held([P, PACK * H], BF16, "w1_bf", bufs=2)
            round_dealt(nc.vector.tensor_copy, rounded, w1_raw[a])
            for i in range(PACK):
                cols = slice(P * i, P * (i + 1))
                quantise(w1_w[:, a, cols], w1_s[:, a, cols], rounded[:, KP * i : KP * (i + 1)])
            for i, c in slots:
                cols = slice(P * i, P * (i + 1))
                nc.tensor.matmul_mx(
                    out=acc[i, c][:],
                    lhsT=w1_w[:, a, cols].bitcast(FP8X4),
                    lhsT_scale=w1_s[:, a, cols],
                    rhs=v_w[a][:, c * BANK : (c + 1) * BANK].bitcast(FP8X4),
                    rhs_scale=v_s[a][:, c * BANK : (c + 1) * BANK],
                    start=(a == 0), stop=(a == PASSES - 1),
                )

        w4_raw, w3_raw, client_raw = {}, {}, {}

        def load_w4(b):
            w4_raw[b] = early.tile([P, PASSES, 2 * KP], U8, name=f"w4_raw{b}", offset=KIB * (26, 40)[b])
            nc.sync.dma_start(
                out=w4_raw[b][:].bitcast(I32),
                in_=w4_words.rearrange("a p c -> p a c")[:, :, 2 * KP * b : 2 * KP * (b + 1)].bitcast(I32),
            )

        def load_client(s):
            for a in range(PASSES):
                client_raw[a, s] = early.tile(
                    [P, PACK, HALF], F32, name=f"client_raw{a}{s}", offset=KIB * ((32, 8)[s] + 4 * a)
                )
                rows_k = client[a * KP : (a + 1) * KP, s * HALF : (s + 1) * HALF]
                nc.sync.dma_start(out=client_raw[a, s][:], in_=rows_k.rearrange("(p j) m -> p j m", j=PACK))

        def load_w3(b):
            w3_raw[b] = early.tile([P, PACK, KP], F32, name=f"w3_raw{b}", offset=KIB * (0, 32)[b])
            nc.sync.dma_start(
                out=w3_raw[b][:], in_=w3[:, b * KP : (b + 1) * KP].rearrange("(p j) n -> p j n", j=PACK)
            )

        load_w4(0)
        load_client(0)
        load_w3(0)
        wgo_sb = early.tile([P, M], F32, name="wgo_sb", offset=44 * KIB)
        nc.sync.dma_start(out=wgo_sb[:], in_=wgo)
        load_client(1)

        w4_w = held([P, 2, PASSES, 2 * KP], U8, "w4_w")
        w3_w = held([P, N], U32, "w3_w")
        w3_s = held([P, N], U8, "w3_s")
        client_w = held([P, PASSES, M], U32, "client_w")
        client_s = held([P, PASSES, M], U8, "client_s")
        x_w = held([P, M], U32, "x_w")
        x_s = held([P, M], U8, "x_s")

        def prepare_w4(b):
            for a in range(PASSES):
                deal(nc.scalar.copy, w4_w[:, b, a, :].bitcast(U16), w4_raw[b][:, a, :].bitcast(U16), 8)

        def prepare_client(s):
            cols = slice(s * HALF, (s + 1) * HALF)
            for a in range(PASSES):
                rounded = held([P, PACK * HALF], BF16, f"client_bf{a}{s}")
                weave(nc.scalar.copy, rounded[:], client_raw[a, s][:])
                quantise(client_w[:, a, cols], client_s[:, a, cols], rounded[:])

        def prepare_w3(b, copy):
            cols = slice(b * KP, (b + 1) * KP)
            rounded = held([P, PACK * KP], BF16, f"w3_bf{b}")
            round_dealt(copy, rounded, w3_raw[b])
            quantise(w3_w[:, cols], w3_s[:, cols], rounded[:])

        x_planes = [held([P, PACK, HALF], BF16, f"x_planes{s}") for s in range(2)]
        for i in range(PACK):
            for c in range(2):
                cols = slice(c * BANK, (c + 1) * BANK)
                nc.vector.tensor_tensor(out=h[i][:, cols], in0=acc[i, c][:], in1=h[i][:, cols], op=ALU.mult)
            for s in range(2):
                picked = held([P, HALF], F32, f"picked{i}{s}")
                nc.vector.tensor_tensor(
                    picked[:],
                    h[i][:].indirect(idx2[:, s * HALF // 16 : (s + 1) * HALF // 16]),
                    wgt_sb[:, s * HALF : (s + 1) * HALF],
                    ALU.mult,
                )
                nc.scalar.activation(
                    out=x_planes[s][:, i, :], in_=picked[:], func=ACT.Identity, bias=shift_sb[:, i : i + 1]
                )
        prepare_w4(0)
        prepare_client(0)
        load_w3(1)
        load_w4(1)
        prepare_w3(0, nc.vector.tensor_copy)
        for s in range(2):
            cols = slice(s * HALF, (s + 1) * HALF)
            x_bf = held([P, PACK * HALF], BF16, f"x_bf{s}")
            weave(nc.vector.tensor_copy, x_bf[:], x_planes[s][:])
            quantise(x_w[:, cols], x_s[:, cols], x_bf[:])

        out_rows = out.rearrange("(b p i) c -> b i p c", b=2, i=PACK)

        def enter(b, i, m0, width, own_sb):
            cols = slice(m0, m0 + width)
            n_cols = slice(b * KP + P * i, b * KP + P * (i + 1))
            own = bank(i, width)
            for a in range(PASSES):
                nc.tensor.matmul_mx(
                    out=own[:],
                    lhsT=w4_w[:, b, a, 2 * P * i : 2 * P * (i + 1)].bitcast(FP4X4),
                    lhsT_scale=w4_s[a][:, n_cols],
                    rhs=client_w[:, a, cols].bitcast(FP8X4),
                    rhs_scale=client_s[:, a, cols],
                    start=(a == 0), stop=(a == PASSES - 1),
                )
            nc.scalar.copy(out=own_sb[:], in_=own[:])
            filed = bank(PACK + i, width)
            nc.tensor.matmul_mx(
                out=filed[:],
                lhsT=w3_w[:, n_cols].bitcast(FP8X4), lhsT_scale=w3_s[:, n_cols],
                rhs=x_w[:, cols].bitcast(FP8X4), rhs_scale=x_s[:, cols],
                start=True, stop=True,
            )
            y = held([P, width], F32, "y", bufs=3)
            nc.vector.tensor_tensor(out=y[:], in0=filed[:], in1=own_sb[:], op=ALU.max)
            nc.vector.tensor_tensor(
                pages[b, i][:].indirect(idx3[:, m0 // 16 : (m0 + width) // 16]), y[:], wgo_sb[:, cols], ALU.mult
            )

        for s in range(2):
            if s == 1:
                prepare_client(1)
            for i in range(PACK):
                own_sb = held([P, HALF], F32, f"own0{i}{s}")
                enter(0, i, s * HALF, HALF, own_sb)
                if s == 1:
                    nc.sync.dma_start(out=out_rows[0, i], in_=pages[0, i][:])
        prepare_w4(1)
        prepare_w3(1, nc.scalar.copy)
        for i in range(PACK):
            own_sb = early.tile([P, M], F32, name=f"own1{i}", offset=2 * KIB * i)
            enter(1, i, 0, M, own_sb)
            nc.sync.dma_start(out=out_rows[1, i], in_=pages[1, i][:])
